import numpy as np
import ml_dtypes


def mxq(x, axis, fmt="e4m3"):
    dtype, down = {"e4m3": (ml_dtypes.float8_e4m3fn, 7), "e5m2": (ml_dtypes.float8_e5m2, 14)}[fmt]
    v = np.moveaxis(np.asarray(x, np.float32).astype(ml_dtypes.bfloat16).astype(np.float64), axis, -1)
    blocks = v.reshape(v.shape[:-1] + (-1, 32))
    amax = np.abs(blocks).max(-1, keepdims=True)
    byte = np.maximum(np.where(amax > 0, np.frexp(amax)[1] - 1 + 127, 0) - down, 1)
    scale = np.exp2(byte - 127.0)
    codes = (blocks / scale).astype(np.float32).astype(dtype).astype(np.float64)
    return np.moveaxis((codes * scale).reshape(v.shape), -1, axis)


WIDE = False


def mx_kscale(k):
    if not WIDE:
        return np.ones(k)
    levels = np.array([10, -10, 5, -5, 0])
    if k % 512:
        return np.exp2(np.random.permutation(np.resize(levels, k // 32))).repeat(32)
    a = np.empty((k // 512, 16))
    for p in range(k // 512):
        a[p, :8] = np.random.permutation(np.resize(levels, 8))
        for g in range(8):
            far = levels[np.abs(levels - a[p, g]) >= 10]
            a[p, g + 8] = far[np.random.randint(len(far))]
    return np.exp2(a.ravel()).repeat(32)


BF16 = ml_dtypes.bfloat16


def bf(x):
    return np.asarray(x, np.float32).astype(BF16)


def f64(x):
    return np.asarray(x).astype(np.float64)

def planes(Y):
    n, m = Y.shape
    b = f64(bf(Y)).reshape(n // 32, 32, m)
    amax = np.abs(b).max(1)
    byte = np.clip(np.where(amax > 0, np.frexp(amax)[1] - 1 + 127 - 7, 1), 1, 254)
    codes = (b * np.exp2(127.0 - byte)[:, None, :]).reshape(n, m).astype(np.float32).astype(ml_dtypes.float8_e4m3fn).view(np.uint8)
    words = codes.reshape(n // 512, 128, 4, m).transpose(0, 1, 3, 2)
    return np.ascontiguousarray(words), np.ascontiguousarray(byte.astype(np.uint8).reshape(n // 512, 16, m))


VIS, SAMP, HID = 2048, 1024, 1536

VIS_STD = 1.0
X_STD = 0.8
BIAS_STD = 0.5
LEVEL_SPREAD = 0.7


def setup_inputs():
    s = mx_kscale(VIS)
    visible = VIS_STD * np.random.randn(VIS, SAMP) * s[:, None]
    coupling = X_STD * np.random.randn(VIS, HID) / np.sqrt(VIS) / s[:, None]
    hidden_bias = BIAS_STD * np.random.randn(HID)
    level = np.exp(LEVEL_SPREAD * np.random.randn(HID))
    return {"visible": bf(visible), "coupling": bf(coupling),
            "hidden_bias": bf(hidden_bias), "level": bf(level)}


def reference(visible, coupling, hidden_bias, level):
    c = f64(hidden_bias)[:, None]
    a = f64(level)[:, None]
    x = mxq(f64(coupling), 0, "e4m3").T @ mxq(f64(visible), 0, "e4m3")
    y = a * (1.0 / (1.0 + np.exp(-(a * (x + c)))))
    Y = y.reshape(HID, SAMP)
    words, scales = planes(Y)
    return y, words, scales

@@ -1,0 +1,176 @@
+from contextlib import ExitStack
+
+import concourse.mybir as mybir
+
+VIS, SAMP, HID = 2048, 1024, 1536
+FLOPS = 2 * VIS * SAMP * HID
+
+F32 = mybir.dt.float32
+BF16 = mybir.dt.bfloat16
+U32 = mybir.dt.uint32
+I32 = mybir.dt.int32
+U8 = mybir.dt.uint8
+FP8X4 = mybir.dt.float8_e4m3fn_x4
+ACT = mybir.ActivationFunctionType
+ALU = mybir.AluOpType
+
+P = 128
+PACK = 4
+SPAN = 512
+UNITS = ["00", "10", "01", "11", "20", "21"]
+
+VQ = "K IW00 QW00 IW10 QX00 QW10 IW20 QX10 QW20 IW30 QX20 QW30 IW01 QX30 QW01 IW11 QX01 QW11 IW21 U000 U001 U002 U003 QW21 IW31 QX11 QW31 IW02 QX21 QW02 IW12 QX31 U100 U101 U102 U103 QW12 IW22 U010 U011 U012 U013 QW22 IW32 C000 QW32 C001 U110 U111 U112 U113 R00 C100 C010 R10 U200 U201 U202 U203 R01 C110 C111 C200 R11 U210 U211 U212 U213 R20 C210 R21".split()
+SQ = "IX00 IX10 IX20 IX30 IX01 A000 A001 A002 A003 IX11 IX21 IX31 A100 A101 A102 A103 A010 A011 A012 A013 A110 A111 A112 A113 C101 C011 A200 A201 A202 A203 C201 A210 A211 A212 A213 C211".split()
+PQ = "M0000 M0001 M0002 M0003 M0010 M0011 M0012 M0013 M0020 M0021 M0022 M0023 M0030 M0031 M0032 M0033 M1000 M1001 M1002 M1003 M1010 M1011 M1012 M1013 M0100 M0101 M0102 M0103 M1020 M1021 M1022 M1023 M0110 M0111 M0112 M0113 M1030 M1031 M1032 M1033 M0120 M0121 M0122 M0123 M0130 M0131 M0132 M0133 M1100 M1110 M1120 M1130 M1101 M1111 M1121 M1131 M1102 M1112 M1122 M1132 M1103 M1113 M1123 M1133 M2000 M2010 M2020 M2030 M2001 M2011 M2021 M2031 M2002 M2012 M2022 M2032 M2003 M2013 M2023 M2033 M2100 M2110 M2120 M2130 M2101 M2111 M2121 M2131 M2102 M2112 M2122 M2132 M2103 M2113 M2123 M2133".split()
+DQ = "LW00 LX00 LW10 LX10 LW20 LX20 LW30 LX30 LW01 LX01 LW11 LX11 LW21 LX21 LW31 LX31 LW02 LW12 LW22 LW32 Y000 Y001 Y100 Y101 Y010 Y011 Y110 Y111 W00 W10 Y200 Y201 W01 Z0 W11 Z1 Y210 Y211 W20 W21 Z2".split()
+
+
+def needs(op):
+    k = op[0]
+    if k == "L":
+        return []
+    if k == "I":
+        return ["L" + op[1:]]
+    if k == "Q":
+        return ["I" + op[1:]]
+    if k == "M":
+        G, n, g, t = op[1], op[2], op[3], op[4]
+        d = ["QX" + g + n, "QW" + g + G]
+        i = UNITS.index(G + n)
+        if g != "0":
+            d.append("M" + G + n + str(int(g) - 1) + t)
+        elif i >= 2:
+            d.append("A" + UNITS[i - 2] + t)
+        return d
+    if k == "A":
+        return ["M" + op[1:3] + "3" + op[3], "K"]
+    if k == "U":
+        return ["A" + op[1:]]
+    if k == "Y":
+        h = int(op[3])
+        return ["U" + op[1:3] + str(2 * h), "U" + op[1:3] + str(2 * h + 1)]
+    if k == "C":
+        return ["U" + op[1:3] + str(t) for t in range(4)]
+    if k == "R":
+        return ["C" + op[1:] + "0", "C" + op[1:] + "1"]
+    if k == "W":
+        return ["R" + op[1:]]
+    if k == "Z":
+        return ["R" + op[1] + "0", "R" + op[1] + "1"]
+    return []
+
+
+def tile_rbm_hidden_means_g2_kernel(tc, visible, coupling, hidden_bias, level, out_0, out_1, out_2):
+    nc = tc.nc
+    with ExitStack() as ctx:
+        keep = ctx.enter_context(tc.tile_pool(name="keep", bufs=1))
+        ring = ctx.enter_context(tc.tile_pool(name="ring", bufs=3))
+        psum = ctx.enter_context(tc.psum_pool(name="psum", bufs=1))
+        ctx.enter_context(tc.manual_schedule())
+
+        raw, codes, scales, grouped, ys, ybs = {}, {}, {}, {}, {}, {}
+        for g in range(4):
+            for key in ["X%d%d" % (g, n) for n in range(2)] + ["W%d%d" % (g, G) for G in range(3)]:
+                raw[key] = keep.tile([P, PACK, SPAN], BF16, name="raw" + key, align_bytes=64)
+                codes[key] = keep.tile([P, SPAN], U32, name="codes" + key, align_bytes=64)
+                scales[key] = keep.tile([P, SPAN], U8, name="scales" + key, align_bytes=64)
+        for u in UNITS:
+            ys[u] = keep.tile([P, PACK, SPAN], F32, name="y" + u, align_bytes=64)
+        ycodes = [keep.tile([P, SAMP], U32, name="ycodes%d" % G, align_bytes=64) for G in range(3)]
+        yscales = [keep.tile([P, SAMP], U8, name="yscales%d" % G, align_bytes=64) for G in range(3)]
+        banks = [psum.tile([P, SPAN], F32, name="bank%d" % b) for b in range(8)]
+        level_bf = keep.tile([P, 3, PACK], BF16, name="level_bf")
+        bias_bf = keep.tile([P, 3, PACK], BF16, name="bias_bf")
+        gain = keep.tile([P, 3, PACK], F32, name="gain")
+        shift = keep.tile([P, 3, PACK], F32, name="shift")
+
+        nc.scalar.dma_start(out=level_bf[:], in_=level.rearrange("(g p t) -> p g t", p=P, t=PACK))
+        nc.scalar.dma_start(out=bias_bf[:], in_=hidden_bias.rearrange("(g p t) -> p g t", p=P, t=PACK))
+
+        def copy(eng, out, in_):
+            if eng == "V":
+                nc.vector.tensor_copy(out=out, in_=in_)
+            else:
+                nc.scalar.copy(out=out, in_=in_)
+
+        def emit(op, eng):
+            k = op[0]
+            if k == "K":
+                nc.vector.tensor_copy(out=gain[:], in_=level_bf[:])
+                nc.vector.tensor_tensor(out=shift[:], in0=level_bf[:], in1=bias_bf[:], op=ALU.mult)
+            elif k == "L":
+                key = op[1:]
+                g, c = int(key[1]), int(key[2])
+                src = visible if key[0] == "X" else coupling
+                rows = src[g * SPAN:(g + 1) * SPAN, c * SPAN:(c + 1) * SPAN]
+                nc.sync.dma_start(out=raw[key][:], in_=rows.rearrange("(p j) w -> p j w", j=PACK))
+            elif k == "I":
+                key = op[1:]
+                grouped[key] = ring.tile([P, PACK * SPAN], BF16, name="grouped" + eng, align_bytes=64)
+                if key[0] == "X":
+                    copy(eng, grouped[key][:].rearrange("p (c i j) -> p c j i", i=4, j=PACK),
+                         raw[key][:].rearrange("p j (c i) -> p c j i", i=4))
+                else:
+                    copy(eng, grouped[key][:].rearrange("p (t m h j) -> p m j h t", t=PACK, h=2, j=PACK),
+                         raw[key][:].rearrange("p j (m h t) -> p m j h t", h=2, t=PACK))
+            elif k == "Q":
+                key = op[1:]
+                nc.vector.quantize_mx(out=codes[key][:].bitcast(FP8X4), scales=scales[key][:], in_=grouped[key][:])
+            elif k == "M":
+                G, n, g, t = op[1], op[2], op[3], int(op[4])
+                bank = banks[4 * (UNITS.index(G + n) % 2) + t]
+                w, x = "W" + g + G, "X" + g + n
+                cols = slice(t * P, (t + 1) * P)
+                nc.tensor.matmul_mx(out=bank[:], lhsT=codes[w][:, cols].bitcast(FP8X4), lhsT_scale=scales[w][:, cols],
+                                    rhs=codes[x][:].bitcast(FP8X4), rhs_scale=scales[x][:],
+                                    start=(g == "0"), stop=(g == "3"))
+            elif k == "A":
+                u, G, t = op[1:3], int(op[1]), int(op[3])
+                bank = banks[4 * (UNITS.index(u) % 2) + t]
+                nc.scalar.activation(out=ys[u][:, t, :], in_=bank[:], func=ACT.Sigmoid,
+                                     scale=gain[:, G, t:t + 1], bias=shift[:, G, t:t + 1])
+            elif k == "U":
+                u, G, t = op[1:3], int(op[1]), int(op[3])
+                if eng == "V":
+                    nc.vector.tensor_scalar(out=ys[u][:, t, :], in0=ys[u][:, t, :], scalar1=gain[:, G, t:t + 1],
+                                            scalar2=None, op0=ALU.mult)
+                else:
+                    nc.scalar.activation(out=ys[u][:, t, :], in_=ys[u][:, t, :], func=ACT.Copy,
+                                         scale=gain[:, G, t:t + 1])
+            elif k == "Y":
+                u, G, n, h = op[1:3], int(op[1]), int(op[2]), int(op[3])
+                dst = out_0[G * SPAN:(G + 1) * SPAN, n * SPAN:(n + 1) * SPAN].rearrange("(p t) m -> p t m", t=PACK)
+                nc.sync.dma_start(out=dst[:, 2 * h:2 * h + 2, :], in_=ys[u][:, 2 * h:2 * h + 2, :])
+            elif k == "C":
+                u, h = op[1:3], int(op[3])
+                if u not in ybs:
+                    ybs[u] = ring.tile([P, PACK * SPAN], BF16, name="ybf", align_bytes=64)
+                copy(eng, ybs[u][:, h * 1024:(h + 1) * 1024].rearrange("p (c i t) -> p c t i", i=4, t=PACK),
+                     ys[u][:, :, h * 256:(h + 1) * 256].rearrange("p t (c i) -> p c t i", i=4))
+            elif k == "R":
+                u, G, n = op[1:3], int(op[1]), int(op[2])
+                cols = slice(n * SPAN, (n + 1) * SPAN)
+                nc.vector.quantize_mx(out=ycodes[G][:, cols].bitcast(FP8X4), scales=yscales[G][:, cols], in_=ybs[u][:])
+            elif k == "W":
+                G, n = int(op[1]), int(op[2])
+                dst = out_1[G].rearrange("p m t -> p (m t)")[:, n * SPAN * PACK:(n + 1) * SPAN * PACK]
+                nc.sync.dma_start(out=dst.bitcast(I32), in_=ycodes[G][:, n * SPAN:(n + 1) * SPAN].bitcast(I32))
+            elif k == "Z":
+                G = int(op[1])
+                for q in range(4):
+                    nc.sync.dma_start(out=out_2[G, 4 * q:4 * q + 4, :].bitcast(I32),
+                                      in_=yscales[G][32 * q:32 * q + 4, :].bitcast(I32))
+
+        queues = {"D": DQ, "V": VQ, "S": SQ, "P": PQ}
+        at = {e: 0 for e in queues}
+        done = set()
+        while any(at[e] < len(queues[e]) for e in queues):
+            moved = False
+            for e in queues:
+                if at[e] < len(queues[e]) and all(d in done for d in needs(queues[e][at[e]])):
+                    op = queues[e][at[e]]
+                    emit(op, e)
+                    done.add(op)
+                    at[e] += 1
+                    moved = True
+            assert moved

@@ -19,10 +19,10 @@ PACK = 4
 SPAN = 512
 UNITS = ["00", "10", "01", "11", "20", "21"]
 
-VQ = "K IW00 QW00 IW10 QX00 QW10 IW20 QX10 QW20 IW30 QX20 QW30 IW01 QX30 QW01 IW11 QX01 QW11 IW21 U000 U001 U002 U003 QW21 IW31 QX11 QW31 IW02 QX21 QW02 IW12 QX31 U100 U101 U102 U103 QW12 IW22 U010 U011 U012 U013 QW22 IW32 C000 QW32 C001 U110 U111 U112 U113 R00 C100 C010 R10 U200 U201 U202 U203 R01 C110 C111 C200 R11 U210 U211 U212 U213 R20 C210 R21".split()
-SQ = "IX00 IX10 IX20 IX30 IX01 A000 A001 A002 A003 IX11 IX21 IX31 A100 A101 A102 A103 A010 A011 A012 A013 A110 A111 A112 A113 C101 C011 A200 A201 A202 A203 C201 A210 A211 A212 A213 C211".split()
+VQ = "IW00 QX00 QW00 IW10 QX10 QW10 IW20 QX20 QW20 IW30 QX30 QW30 IX01 QW01 IW11 U000 U001 U002 U003 QW11 QX01 IX11 QW21 IX21 QX11 QW31 IW02 QX21 QX31 IW12 IW22 U100 U101 U102 U103 QW02 U010 U011 U012 U013 QW12 QW22 QW32 C000 U110 U111 U112 U113 C001 C010 R00 R01 C110 U200 U201 U202 U203 C200 C100 C101 R11 R10 C201 U212 U213 C210 R20 r210 r211".split()
+SQ = "IX00 IX10 IX20 IX30 IW01 A000 A001 A002 A003 IW21 IW31 IX31 A100 A101 A102 A103 A010 A011 A012 A013 IW32 A110 A111 A112 A113 C011 A200 A201 A202 A203 C111 A210 A211 U210 U211 A212 A213 C211 Z2".split()
 PQ = "M0000 M0001 M0002 M0003 M0010 M0011 M0012 M0013 M0020 M0021 M0022 M0023 M0030 M0031 M0032 M0033 M1000 M1001 M1002 M1003 M1010 M1011 M1012 M1013 M0100 M0101 M0102 M0103 M1020 M1021 M1022 M1023 M0110 M0111 M0112 M0113 M1030 M1031 M1032 M1033 M0120 M0121 M0122 M0123 M0130 M0131 M0132 M0133 M1100 M1110 M1120 M1130 M1101 M1111 M1121 M1131 M1102 M1112 M1122 M1132 M1103 M1113 M1123 M1133 M2000 M2010 M2020 M2030 M2001 M2011 M2021 M2031 M2002 M2012 M2022 M2032 M2003 M2013 M2023 M2033 M2100 M2110 M2120 M2130 M2101 M2111 M2121 M2131 M2102 M2112 M2122 M2132 M2103 M2113 M2123 M2133".split()
-DQ = "LW00 LX00 LW10 LX10 LW20 LX20 LW30 LX30 LW01 LX01 LW11 LX11 LW21 LX21 LW31 LX31 LW02 LW12 LW22 LW32 Y000 Y001 Y100 Y101 Y010 Y011 Y110 Y111 W00 W10 Y200 Y201 W01 Z0 W11 Z1 Y210 Y211 W20 W21 Z2".split()
+DQ = "LX00 LW00 LX10 LW10 LX20 LW20 LX30 LW30 LW01 LX01 LW11 LX11 LW21 LX21 LW31 LX31 LW02 LW12 LW22 LW32 Y000 Y001 Y100 Y101 Y010 Y011 Y110 Y111 W0 Y200 Y201 y210 y211 W1 Z01 y212 y213 W20 w210 w211".split()
 
 
 def needs(op):
@@ -43,7 +43,7 @@ def needs(op):
             d.append("A" + UNITS[i - 2] + t)
         return d
     if k == "A":
-        return ["M" + op[1:3] + "3" + op[3], "K"]
+        return ["M" + op[1:3] + "3" + op[3]]
     if k == "U":
         return ["A" + op[1:]]
     if k == "Y":
@@ -53,10 +53,18 @@ def needs(op):
         return ["U" + op[1:3] + str(t) for t in range(4)]
     if k == "R":
         return ["C" + op[1:] + "0", "C" + op[1:] + "1"]
+    if k == "y":
+        return ["U" + op[1:]]
+    if k == "r":
+        return ["C" + op[1:]]
+    if k == "w":
+        return ["r" + op[1:]]
     if k == "W":
-        return ["R" + op[1:]]
-    if k == "Z":
-        return ["R" + op[1] + "0", "R" + op[1] + "1"]
+        return ["R" + op[1:]] if len(op) == 3 else ["R" + op[1] + "0", "R" + op[1] + "1"]
+    if op == "Z01":
+        return ["R00", "R01", "R10", "R11"]
+    if op == "Z2":
+        return ["R20", "r210", "r211"]
     return []
 
 
@@ -64,28 +72,37 @@ def tile_rbm_hidden_means_g2_kernel(tc, visible, coupling, hidden_bias, level, o
     nc = tc.nc
     with ExitStack() as ctx:
         keep = ctx.enter_context(tc.tile_pool(name="keep", bufs=1))
-        ring = ctx.enter_context(tc.tile_pool(name="ring", bufs=3))
+        ring = ctx.enter_context(tc.tile_pool(name="ring", bufs=4))
+        loads = ctx.enter_context(tc.tile_pool(name="loads", bufs=12))
         psum = ctx.enter_context(tc.psum_pool(name="psum", bufs=1))
         ctx.enter_context(tc.manual_schedule())
 
         raw, codes, scales, grouped, ys, ybs = {}, {}, {}, {}, {}, {}
         for g in range(4):
             for key in ["X%d%d" % (g, n) for n in range(2)] + ["W%d%d" % (g, G) for G in range(3)]:
-                raw[key] = keep.tile([P, PACK, SPAN], BF16, name="raw" + key, align_bytes=64)
                 codes[key] = keep.tile([P, SPAN], U32, name="codes" + key, align_bytes=64)
                 scales[key] = keep.tile([P, SPAN], U8, name="scales" + key, align_bytes=64)
         for u in UNITS:
+            ybs[u] = keep.tile([P, PACK * SPAN], BF16, name="ybf" + u, align_bytes=64)
             ys[u] = keep.tile([P, PACK, SPAN], F32, name="y" + u, align_bytes=64)
         ycodes = [keep.tile([P, SAMP], U32, name="ycodes%d" % G, align_bytes=64) for G in range(3)]
-        yscales = [keep.tile([P, SAMP], U8, name="yscales%d" % G, align_bytes=64) for G in range(3)]
+        ysc01 = keep.tile([P, 2, SAMP], U8, name="ysc01", align_bytes=64)
+        ysc2 = keep.tile([P, SAMP], U8, name="ysc2", align_bytes=64)
+        yscales = [ysc01[:, 0, :], ysc01[:, 1, :], ysc2[:]]
         banks = [psum.tile([P, SPAN], F32, name="bank%d" % b) for b in range(8)]
         level_bf = keep.tile([P, 3, PACK], BF16, name="level_bf")
         bias_bf = keep.tile([P, 3, PACK], BF16, name="bias_bf")
         gain = keep.tile([P, 3, PACK], F32, name="gain")
         shift = keep.tile([P, 3, PACK], F32, name="shift")
+        warm_in = keep.tile([P, 1], F32, name="warm_in")
+        warm_out = keep.tile([P, 1], F32, name="warm_out")
+        nc.vector.memset(warm_in[:], 0.0)
 
         nc.scalar.dma_start(out=level_bf[:], in_=level.rearrange("(g p t) -> p g t", p=P, t=PACK))
         nc.scalar.dma_start(out=bias_bf[:], in_=hidden_bias.rearrange("(g p t) -> p g t", p=P, t=PACK))
+        nc.scalar.activation(out=warm_out[:], in_=warm_in[:], func=ACT.Sigmoid)
+        nc.gpsimd.tensor_copy(out=gain[:], in_=level_bf[:])
+        nc.gpsimd.tensor_tensor(out=shift[:], in0=level_bf[:], in1=bias_bf[:], op=ALU.mult)
 
         def copy(eng, out, in_):
             if eng == "V":
@@ -95,14 +112,12 @@ def tile_rbm_hidden_means_g2_kernel(tc, visible, coupling, hidden_bias, level, o
 
         def emit(op, eng):
             k = op[0]
-            if k == "K":
-                nc.vector.tensor_copy(out=gain[:], in_=level_bf[:])
-                nc.vector.tensor_tensor(out=shift[:], in0=level_bf[:], in1=bias_bf[:], op=ALU.mult)
-            elif k == "L":
+            if k == "L":
                 key = op[1:]
                 g, c = int(key[1]), int(key[2])
                 src = visible if key[0] == "X" else coupling
                 rows = src[g * SPAN:(g + 1) * SPAN, c * SPAN:(c + 1) * SPAN]
+                raw[key] = loads.tile([P, PACK, SPAN], BF16, name="raw", align_bytes=64)
                 nc.sync.dma_start(out=raw[key][:], in_=rows.rearrange("(p j) w -> p j w", j=PACK))
             elif k == "I":
                 key = op[1:]
@@ -111,8 +126,8 @@ def tile_rbm_hidden_means_g2_kernel(tc, visible, coupling, hidden_bias, level, o
                     copy(eng, grouped[key][:].rearrange("p (c i j) -> p c j i", i=4, j=PACK),
                          raw[key][:].rearrange("p j (c i) -> p c j i", i=4))
                 else:
-                    copy(eng, grouped[key][:].rearrange("p (t m h j) -> p m j h t", t=PACK, h=2, j=PACK),
-                         raw[key][:].rearrange("p j (m h t) -> p m j h t", h=2, t=PACK))
+                    copy(eng, grouped[key][:].rearrange("p (t m h j) -> p m j t h", t=PACK, h=2, j=PACK),
+                         raw[key][:].rearrange("p j (m h t) -> p m j t h", h=2, t=PACK))
             elif k == "Q":
                 key = op[1:]
                 nc.vector.quantize_mx(out=codes[key][:].bitcast(FP8X4), scales=scales[key][:], in_=grouped[key][:])
@@ -143,23 +158,38 @@ def tile_rbm_hidden_means_g2_kernel(tc, visible, coupling, hidden_bias, level, o
                 nc.sync.dma_start(out=dst[:, 2 * h:2 * h + 2, :], in_=ys[u][:, 2 * h:2 * h + 2, :])
             elif k == "C":
                 u, h = op[1:3], int(op[3])
-                if u not in ybs:
-                    ybs[u] = ring.tile([P, PACK * SPAN], BF16, name="ybf", align_bytes=64)
                 copy(eng, ybs[u][:, h * 1024:(h + 1) * 1024].rearrange("p (c i t) -> p c t i", i=4, t=PACK),
                      ys[u][:, :, h * 256:(h + 1) * 256].rearrange("p t (c i) -> p c t i", i=4))
             elif k == "R":
                 u, G, n = op[1:3], int(op[1]), int(op[2])
                 cols = slice(n * SPAN, (n + 1) * SPAN)
                 nc.vector.quantize_mx(out=ycodes[G][:, cols].bitcast(FP8X4), scales=yscales[G][:, cols], in_=ybs[u][:])
-            elif k == "W":
-                G, n = int(op[1]), int(op[2])
-                dst = out_1[G].rearrange("p m t -> p (m t)")[:, n * SPAN * PACK:(n + 1) * SPAN * PACK]
-                nc.sync.dma_start(out=dst.bitcast(I32), in_=ycodes[G][:, n * SPAN:(n + 1) * SPAN].bitcast(I32))
-            elif k == "Z":
+            elif k == "y":
+                u, G, n, t = op[1:3], int(op[1]), int(op[2]), int(op[3])
+                dst = out_0[G * SPAN:(G + 1) * SPAN, n * SPAN:(n + 1) * SPAN].rearrange("(p t) m -> p t m", t=PACK)
+                nc.sync.dma_start(out=dst[:, t, :], in_=ys[u][:, t, :])
+            elif k == "r":
+                u, G, n, h = op[1:3], int(op[1]), int(op[2]), int(op[3])
+                cols = slice(n * SPAN + h * 256, n * SPAN + (h + 1) * 256)
+                nc.vector.quantize_mx(out=ycodes[G][:, cols].bitcast(FP8X4), scales=yscales[G][:, cols],
+                                      in_=ybs[u][:, h * 1024:(h + 1) * 1024])
+            elif k in "Ww":
                 G = int(op[1])
+                lo, hi = 0, SAMP
+                if len(op) > 2:
+                    lo, hi = int(op[2]) * SPAN, (int(op[2]) + 1) * SPAN
+                if len(op) > 3:
+                    lo, hi = lo + int(op[3]) * 256, lo + (int(op[3]) + 1) * 256
+                dst = out_1[G].rearrange("p m t -> p (m t)")[:, lo * PACK:hi * PACK]
+                nc.sync.dma_start(out=dst.bitcast(I32), in_=ycodes[G][:, lo:hi].bitcast(I32))
+            elif op == "Z01":
                 for q in range(4):
-                    nc.sync.dma_start(out=out_2[G, 4 * q:4 * q + 4, :].bitcast(I32),
-                                      in_=yscales[G][32 * q:32 * q + 4, :].bitcast(I32))
+                    nc.sync.dma_start(out=out_2[0:2, 4 * q:4 * q + 4, :].rearrange("g r m -> r g m").bitcast(I32),
+                                      in_=ysc01[32 * q:32 * q + 4, :, :].bitcast(I32))
+            elif op == "Z2":
+                for q in range(4):
+                    nc.scalar.dma_start(out=out_2[2, 4 * q:4 * q + 4, :].bitcast(I32),
+                                        in_=ysc2[32 * q:32 * q + 4, :].bitcast(I32))
 
         queues = {"D": DQ, "V": VQ, "S": SQ, "P": PQ}
         at = {e: 0 for e in queues}

@@ -1,6 +1,7 @@
 from contextlib import ExitStack
 
 import concourse.mybir as mybir
+from concourse.masks import make_identity
 
 VIS, SAMP, HID = 2048, 1024, 1536
 FLOPS = 2 * VIS * SAMP * HID
@@ -19,10 +20,10 @@ PACK = 4
 SPAN = 512
 UNITS = ["00", "10", "01", "11", "20", "21"]
 
-VQ = "IW00 QX00 QW00 IW10 QX10 QW10 IW20 QX20 QW20 IW30 QX30 QW30 IX01 QW01 IW11 U000 U001 U002 U003 QW11 QX01 IX11 QW21 IX21 QX11 QW31 IW02 QX21 QX31 IW12 IW22 U100 U101 U102 U103 QW02 U010 U011 U012 U013 QW12 QW22 QW32 C000 U110 U111 U112 U113 C001 C010 R00 R01 C110 U200 U201 U202 U203 C200 C100 C101 R11 R10 C201 U212 U213 C210 R20 r210 r211".split()
-SQ = "IX00 IX10 IX20 IX30 IW01 A000 A001 A002 A003 IW21 IW31 IX31 A100 A101 A102 A103 A010 A011 A012 A013 IW32 A110 A111 A112 A113 C011 A200 A201 A202 A203 C111 A210 A211 U210 U211 A212 A213 C211 Z2".split()
-PQ = "M0000 M0001 M0002 M0003 M0010 M0011 M0012 M0013 M0020 M0021 M0022 M0023 M0030 M0031 M0032 M0033 M1000 M1001 M1002 M1003 M1010 M1011 M1012 M1013 M0100 M0101 M0102 M0103 M1020 M1021 M1022 M1023 M0110 M0111 M0112 M0113 M1030 M1031 M1032 M1033 M0120 M0121 M0122 M0123 M0130 M0131 M0132 M0133 M1100 M1110 M1120 M1130 M1101 M1111 M1121 M1131 M1102 M1112 M1122 M1132 M1103 M1113 M1123 M1133 M2000 M2010 M2020 M2030 M2001 M2011 M2021 M2031 M2002 M2012 M2022 M2032 M2003 M2013 M2023 M2033 M2100 M2110 M2120 M2130 M2101 M2111 M2121 M2131 M2102 M2112 M2122 M2132 M2103 M2113 M2123 M2133".split()
-DQ = "LX00 LW00 LX10 LW10 LX20 LW20 LX30 LW30 LW01 LX01 LW11 LX11 LW21 LX21 LW31 LX31 LW02 LW12 LW22 LW32 Y000 Y001 Y100 Y101 Y010 Y011 Y110 Y111 W0 Y200 Y201 y210 y211 W1 Z01 y212 y213 W20 w210 w211".split()
+VQ = "IW00 QX00 QW00 IW10 QX10 QW10 IW20 QX20 QW20 IW30 QX30 K QW30 k IX01 QW01 IW11 QX01 QW11 IX11 QW21 IX21 QX11 QW31 QX21 U000 U001 U002 U003 QX31 IW02 U100 U101 U102 U103 IW22 QW02 IW32 QW12 U010 U011 U012 U013 QW22 QW32 U110 U111 U112 U113 C000 C001 C010 U200 U201 U202 U203 R00 C110 R01 C101 R11 R10 U210 U211 C200 U212 U213 C210 R20 r210 r211".split()
+SQ = "IX00 IX10 IX20 IX30 IW01 A000 A001 A002 A003 IW21 IW31 IX31 A100 A101 A102 A103 IW12 A010 A011 A012 A013 A110 A111 A112 A113 C011 A200 A201 A202 A203 C100 C111 A210 A211 A212 A213 C201 C211 Z2".split()
+PQ = "M0000 M0001 M0002 M0003 M0010 M0011 M0012 M0013 M0020 M0021 M0022 M0023 T M0030 M0031 M0032 M0033 M1000 M1001 M1002 M1003 M1010 M1011 M1012 M1013 M0100 M0101 M0102 M0103 M1020 M1021 M1022 M1023 M0110 M0111 M0112 M0113 M1030 M1031 M1032 M1033 M0120 M0121 M0122 M0123 M1100 M1110 M1101 M1111 M1102 M1112 M1103 M1113 M0130 M0131 M0132 M0133 M1120 M1130 M1121 M1131 M1122 M1132 M1123 M1133 M2000 M2010 M2001 M2011 M2002 M2012 M2003 M2013 M2020 M2030 M2021 M2031 M2022 M2032 M2023 M2033 M2100 M2110 M2120 M2130 M2101 M2111 M2121 M2131 M2102 M2112 M2122 M2132 M2103 M2113 M2123 M2133".split()
+DQ = "LX00 LW00 LX10 LW10 LX20 LW20 LX30 LW30 LW01 LX01 LW11 LW21 LX11 LW31 LX21 LX31 LW02 LW12 LW22 LW32 Y000 Y001 Y100 Y101 Y010 Y011 Y110 Y111 Y200 Y201 W0 W1 Z01 Y210 Y211 W2a w211".split()
 
 
 def needs(op):
@@ -37,13 +38,15 @@ def needs(op):
         G, n, g, t = op[1], op[2], op[3], op[4]
         d = ["QX" + g + n, "QW" + g + G]
         i = UNITS.index(G + n)
+        if g == "0" and i == 1:
+            d.append("k")
         if g != "0":
             d.append("M" + G + n + str(int(g) - 1) + t)
         elif i >= 2:
             d.append("A" + UNITS[i - 2] + t)
         return d
     if k == "A":
-        return ["M" + op[1:3] + "3" + op[3]]
+        return ["M" + op[1:3] + "3" + op[3], "k"]
     if k == "U":
         return ["A" + op[1:]]
     if k == "Y":
@@ -53,6 +56,10 @@ def needs(op):
         return ["U" + op[1:3] + str(t) for t in range(4)]
     if k == "R":
         return ["C" + op[1:] + "0", "C" + op[1:] + "1"]
+    if k == "K":
+        return ["T"]
+    if op == "W2a":
+        return ["R20", "r210"]
     if k == "y":
         return ["U" + op[1:]]
     if k == "r":
@@ -90,19 +97,21 @@ def tile_rbm_hidden_means_g2_kernel(tc, visible, coupling, hidden_bias, level, o
         ysc2 = keep.tile([P, SAMP], U8, name="ysc2", align_bytes=64)
         yscales = [ysc01[:, 0, :], ysc01[:, 1, :], ysc2[:]]
         banks = [psum.tile([P, SPAN], F32, name="bank%d" % b) for b in range(8)]
-        level_bf = keep.tile([P, 3, PACK], BF16, name="level_bf")
-        bias_bf = keep.tile([P, 3, PACK], BF16, name="bias_bf")
+        rows_bf = keep.tile([P, SPAN], BF16, name="rows_bf", align_bytes=64)
+        ident = keep.tile([P, P], F32, name="ident", align_bytes=64)
         gain = keep.tile([P, 3, PACK], F32, name="gain")
         shift = keep.tile([P, 3, PACK], F32, name="shift")
         warm_in = keep.tile([P, 1], F32, name="warm_in")
         warm_out = keep.tile([P, 1], F32, name="warm_out")
         nc.vector.memset(warm_in[:], 0.0)
 
-        nc.scalar.dma_start(out=level_bf[:], in_=level.rearrange("(g p t) -> p g t", p=P, t=PACK))
-        nc.scalar.dma_start(out=bias_bf[:], in_=hidden_bias.rearrange("(g p t) -> p g t", p=P, t=PACK))
+        nc.gpsimd.memset(rows_bf[:], 0.0)
+        make_identity(nc, ident[:])
+        nc.gpsimd.dma_start(out=rows_bf[0:3, :], in_=level.rearrange("(g c) -> g c", g=3))
+        nc.gpsimd.dma_start(out=rows_bf[4:7, :], in_=hidden_bias.rearrange("(g c) -> g c", g=3))
+        words = rows_bf[:].bitcast(F32)
+        turned = banks[7][:].bitcast(BF16)[:, 0:4 * P].rearrange("p (u r e) -> p r u e", u=2, e=2)
         nc.scalar.activation(out=warm_out[:], in_=warm_in[:], func=ACT.Sigmoid)
-        nc.gpsimd.tensor_copy(out=gain[:], in_=level_bf[:])
-        nc.gpsimd.tensor_tensor(out=shift[:], in0=level_bf[:], in1=bias_bf[:], op=ALU.mult)
 
         def copy(eng, out, in_):
             if eng == "V":
@@ -112,7 +121,16 @@ def tile_rbm_hidden_means_g2_kernel(tc, visible, coupling, hidden_bias, level, o
 
         def emit(op, eng):
             k = op[0]
-            if k == "L":
+            if k == "T":
+                for u in range(2):
+                    nc.tensor.transpose(banks[7][:, u * P:(u + 1) * P], words[:, u:2 * P:2], ident[:])
+            elif k == "K":
+                nc.vector.tensor_copy(out=gain[:].rearrange("p g (u e) -> p g u e", e=2), in_=turned[:, 0:3, :, :])
+            elif k == "k":
+                nc.vector.tensor_tensor(out=shift[:].rearrange("p g (u e) -> p g u e", e=2),
+                                        in0=gain[:].rearrange("p g (u e) -> p g u e", e=2),
+                                        in1=turned[:, 4:7, :, :], op=ALU.mult)
+            elif k == "L":
                 key = op[1:]
                 g, c = int(key[1]), int(key[2])
                 src = visible if key[0] == "X" else coupling
@@ -126,8 +144,10 @@ def tile_rbm_hidden_means_g2_kernel(tc, visible, coupling, hidden_bias, level, o
                     copy(eng, grouped[key][:].rearrange("p (c i j) -> p c j i", i=4, j=PACK),
                          raw[key][:].rearrange("p j (c i) -> p c j i", i=4))
                 else:
-                    copy(eng, grouped[key][:].rearrange("p (t m h j) -> p m j t h", t=PACK, h=2, j=PACK),
-                         raw[key][:].rearrange("p j (m h t) -> p m j t h", h=2, t=PACK))
+                    src = raw[key][:].rearrange("p j (m h u t) -> p u m j h t", h=2, u=2, t=2)
+                    for u in range(2):
+                        copy(eng, grouped[key][:, u * 1024:(u + 1) * 1024].rearrange("p (t m h j) -> p m j h t", t=2, h=2, j=PACK),
+                             src[:, u, :, :, :, :])
             elif k == "Q":
                 key = op[1:]
                 nc.vector.quantize_mx(out=codes[key][:].bitcast(FP8X4), scales=scales[key][:], in_=grouped[key][:])
@@ -176,7 +196,9 @@ def tile_rbm_hidden_means_g2_kernel(tc, visible, coupling, hidden_bias, level, o
             elif k in "Ww":
                 G = int(op[1])
                 lo, hi = 0, SAMP
-                if len(op) > 2:
+                if op == "W2a":
+                    lo, hi = 0, 768
+                elif len(op) > 2:
                     lo, hi = int(op[2]) * SPAN, (int(op[2]) + 1) * SPAN
                 if len(op) > 3:
                     lo, hi = lo + int(op[3]) * 256, lo + (int(op[3]) + 1) * 256

from contextlib import ExitStack

import concourse.mybir as mybir
from concourse.masks import make_identity

VIS, SAMP, HID = 2048, 1024, 1536
FLOPS = 2 * VIS * SAMP * HID

F32 = mybir.dt.float32
BF16 = mybir.dt.bfloat16
U32 = mybir.dt.uint32
I32 = mybir.dt.int32
U8 = mybir.dt.uint8
FP8X4 = mybir.dt.float8_e4m3fn_x4
ACT = mybir.ActivationFunctionType
ALU = mybir.AluOpType

P = 128
PACK = 4
SPAN = 512
UNITS = ["00", "10", "01", "11", "20", "21"]

VQ = "IW00 QX00 QW00 IW10 QX10 QW10 IW20 QX20 QW20 IW30 QX30 K QW30 k IX01 QW01 IW11 QX01 QW11 IX11 QW21 IX21 QX11 QW31 QX21 U000 U001 U002 U003 QX31 IW02 U100 U101 U102 U103 IW22 QW02 IW32 QW12 U010 U011 U012 U013 QW22 QW32 U110 U111 U112 U113 C000 C001 C010 U200 U201 U202 U203 R00 C110 R01 C101 R11 R10 U210 U211 C200 U212 U213 C210 R20 r210 r211".split()
SQ = "IX00 IX10 IX20 IX30 IW01 A000 A001 A002 A003 IW21 IW31 IX31 A100 A101 A102 A103 IW12 A010 A011 A012 A013 A110 A111 A112 A113 C011 A200 A201 A202 A203 C100 C111 A210 A211 A212 A213 C201 C211 Z2".split()
PQ = "M0000 M0001 M0002 M0003 M0010 M0011 M0012 M0013 M0020 M0021 M0022 M0023 T M0030 M0031 M0032 M0033 M1000 M1001 M1002 M1003 M1010 M1011 M1012 M1013 M0100 M0101 M0102 M0103 M1020 M1021 M1022 M1023 M0110 M0111 M0112 M0113 M1030 M1031 M1032 M1033 M0120 M0121 M0122 M0123 M1100 M1110 M1101 M1111 M1102 M1112 M1103 M1113 M0130 M0131 M0132 M0133 M1120 M1130 M1121 M1131 M1122 M1132 M1123 M1133 M2000 M2010 M2001 M2011 M2002 M2012 M2003 M2013 M2020 M2030 M2021 M2031 M2022 M2032 M2023 M2033 M2100 M2110 M2120 M2130 M2101 M2111 M2121 M2131 M2102 M2112 M2122 M2132 M2103 M2113 M2123 M2133".split()
DQ = "LX00 LW00 LX10 LW10 LX20 LW20 LX30 LW30 LW01 LX01 LW11 LW21 LX11 LW31 LX21 LX31 LW02 LW12 LW22 LW32 Y000 Y001 Y100 Y101 Y010 Y011 Y110 Y111 Y200 Y201 W0 W1 Z01 Y210 Y211 W2a w211".split()


def needs(op):
    k = op[0]
    if k == "L":
        return []
    if k == "I":
        return ["L" + op[1:]]
    if k == "Q":
        return ["I" + op[1:]]
    if k == "M":
        G, n, g, t = op[1], op[2], op[3], op[4]
        d = ["QX" + g + n, "QW" + g + G]
        i = UNITS.index(G + n)
        if g == "0" and i == 1:
            d.append("k")
        if g != "0":
            d.append("M" + G + n + str(int(g) - 1) + t)
        elif i >= 2:
            d.append("A" + UNITS[i - 2] + t)
        return d
    if k == "A":
        return ["M" + op[1:3] + "3" + op[3], "k"]
    if k == "U":
        return ["A" + op[1:]]
    if k == "Y":
        h = int(op[3])
        return ["U" + op[1:3] + str(2 * h), "U" + op[1:3] + str(2 * h + 1)]
    if k == "C":
        return ["U" + op[1:3] + str(t) for t in range(4)]
    if k == "R":
        return ["C" + op[1:] + "0", "C" + op[1:] + "1"]
    if k == "K":
        return ["T"]
    if op == "W2a":
        return ["R20", "r210"]
    if k == "y":
        return ["U" + op[1:]]
    if k == "r":
        return ["C" + op[1:]]
    if k == "w":
        return ["r" + op[1:]]
    if k == "W":
        return ["R" + op[1:]] if len(op) == 3 else ["R" + op[1] + "0", "R" + op[1] + "1"]
    if op == "Z01":
        return ["R00", "R01", "R10", "R11"]
    if op == "Z2":
        return ["R20", "r210", "r211"]
    return []


def tile_rbm_hidden_means_g2_kernel(tc, visible, coupling, hidden_bias, level, out_0, out_1, out_2):
    nc = tc.nc
    with ExitStack() as ctx:
        keep = ctx.enter_context(tc.tile_pool(name="keep", bufs=1))
        ring = ctx.enter_context(tc.tile_pool(name="ring", bufs=4))
        loads = ctx.enter_context(tc.tile_pool(name="loads", bufs=12))
        psum = ctx.enter_context(tc.psum_pool(name="psum", bufs=1))
        ctx.enter_context(tc.manual_schedule())

        raw, codes, scales, grouped, ys, ybs = {}, {}, {}, {}, {}, {}
        for g in range(4):
            for key in ["X%d%d" % (g, n) for n in range(2)] + ["W%d%d" % (g, G) for G in range(3)]:
                codes[key] = keep.tile([P, SPAN], U32, name="codes" + key, align_bytes=64)
                scales[key] = keep.tile([P, SPAN], U8, name="scales" + key, align_bytes=64)
        for u in UNITS:
            ybs[u] = keep.tile([P, PACK * SPAN], BF16, name="ybf" + u, align_bytes=64)
            ys[u] = keep.tile([P, PACK, SPAN], F32, name="y" + u, align_bytes=64)
        ycodes = [keep.tile([P, SAMP], U32, name="ycodes%d" % G, align_bytes=64) for G in range(3)]
        ysc01 = keep.tile([P, 2, SAMP], U8, name="ysc01", align_bytes=64)
        ysc2 = keep.tile([P, SAMP], U8, name="ysc2", align_bytes=64)
        yscales = [ysc01[:, 0, :], ysc01[:, 1, :], ysc2[:]]
        banks = [psum.tile([P, SPAN], F32, name="bank%d" % b) for b in range(8)]
        rows_bf = keep.tile([P, SPAN], BF16, name="rows_bf", align_bytes=64)
        ident = keep.tile([P, P], F32, name="ident", align_bytes=64)
        gain = keep.tile([P, 3, PACK], F32, name="gain")
        shift = keep.tile([P, 3, PACK], F32, name="shift")
        warm_in = keep.tile([P, 1], F32, name="warm_in")
        warm_out = keep.tile([P, 1], F32, name="warm_out")
        nc.vector.memset(warm_in[:], 0.0)

        nc.gpsimd.memset(rows_bf[:], 0.0)
        make_identity(nc, ident[:])
        nc.gpsimd.dma_start(out=rows_bf[0:3, :], in_=level.rearrange("(g c) -> g c", g=3))
        nc.gpsimd.dma_start(out=rows_bf[4:7, :], in_=hidden_bias.rearrange("(g c) -> g c", g=3))
        words = rows_bf[:].bitcast(F32)
        turned = banks[7][:].bitcast(BF16)[:, 0:4 * P].rearrange("p (u r e) -> p r u e", u=2, e=2)
        nc.scalar.activation(out=warm_out[:], in_=warm_in[:], func=ACT.Sigmoid)

        def copy(eng, out, in_):
            if eng == "V":
                nc.vector.tensor_copy(out=out, in_=in_)
            else:
                nc.scalar.copy(out=out, in_=in_)

        def emit(op, eng):
            k = op[0]
            if k == "T":
                for u in range(2):
                    nc.tensor.transpose(banks[7][:, u * P:(u + 1) * P], words[:, u:2 * P:2], ident[:])
            elif k == "K":
                nc.vector.tensor_copy(out=gain[:].rearrange("p g (u e) -> p g u e", e=2), in_=turned[:, 0:3, :, :])
            elif k == "k":
                nc.vector.tensor_tensor(out=shift[:].rearrange("p g (u e) -> p g u e", e=2),
                                        in0=gain[:].rearrange("p g (u e) -> p g u e", e=2),
                                        in1=turned[:, 4:7, :, :], op=ALU.mult)
            elif k == "L":
                key = op[1:]
                g, c = int(key[1]), int(key[2])
                src = visible if key[0] == "X" else coupling
                rows = src[g * SPAN:(g + 1) * SPAN, c * SPAN:(c + 1) * SPAN]
                raw[key] = loads.tile([P, PACK, SPAN], BF16, name="raw", align_bytes=64)
                nc.sync.dma_start(out=raw[key][:], in_=rows.rearrange("(p j) w -> p j w", j=PACK))
            elif k == "I":
                key = op[1:]
                grouped[key] = ring.tile([P, PACK * SPAN], BF16, name="grouped" + eng, align_bytes=64)
                if key[0] == "X":
                    copy(eng, grouped[key][:].rearrange("p (c i j) -> p c j i", i=4, j=PACK),
                         raw[key][:].rearrange("p j (c i) -> p c j i", i=4))
                else:
                    src = raw[key][:].rearrange("p j (m h u t) -> p u m j h t", h=2, u=2, t=2)
                    for u in range(2):
                        copy(eng, grouped[key][:, u * 1024:(u + 1) * 1024].rearrange("p (t m h j) -> p m j h t", t=2, h=2, j=PACK),
                             src[:, u, :, :, :, :])
            elif k == "Q":
                key = op[1:]
                nc.vector.quantize_mx(out=codes[key][:].bitcast(FP8X4), scales=scales[key][:], in_=grouped[key][:])
            elif k == "M":
                G, n, g, t = op[1], op[2], op[3], int(op[4])
                bank = banks[4 * (UNITS.index(G + n) % 2) + t]
                w, x = "W" + g + G, "X" + g + n
                cols = slice(t * P, (t + 1) * P)
                nc.tensor.matmul_mx(out=bank[:], lhsT=codes[w][:, cols].bitcast(FP8X4), lhsT_scale=scales[w][:, cols],
                                    rhs=codes[x][:].bitcast(FP8X4), rhs_scale=scales[x][:],
                                    start=(g == "0"), stop=(g == "3"))
            elif k == "A":
                u, G, t = op[1:3], int(op[1]), int(op[3])
                bank = banks[4 * (UNITS.index(u) % 2) + t]
                nc.scalar.activation(out=ys[u][:, t, :], in_=bank[:], func=ACT.Sigmoid,
                                     scale=gain[:, G, t:t + 1], bias=shift[:, G, t:t + 1])
            elif k == "U":
                u, G, t = op[1:3], int(op[1]), int(op[3])
                if eng == "V":
                    nc.vector.tensor_scalar(out=ys[u][:, t, :], in0=ys[u][:, t, :], scalar1=gain[:, G, t:t + 1],
                                            scalar2=None, op0=ALU.mult)
                else:
                    nc.scalar.activation(out=ys[u][:, t, :], in_=ys[u][:, t, :], func=ACT.Copy,
                                         scale=gain[:, G, t:t + 1])
            elif k == "Y":
                u, G, n, h = op[1:3], int(op[1]), int(op[2]), int(op[3])
                dst = out_0[G * SPAN:(G + 1) * SPAN, n * SPAN:(n + 1) * SPAN].rearrange("(p t) m -> p t m", t=PACK)
                nc.sync.dma_start(out=dst[:, 2 * h:2 * h + 2, :], in_=ys[u][:, 2 * h:2 * h + 2, :])
            elif k == "C":
                u, h = op[1:3], int(op[3])
                copy(eng, ybs[u][:, h * 1024:(h + 1) * 1024].rearrange("p (c i t) -> p c t i", i=4, t=PACK),
                     ys[u][:, :, h * 256:(h + 1) * 256].rearrange("p t (c i) -> p c t i", i=4))
            elif k == "R":
                u, G, n = op[1:3], int(op[1]), int(op[2])
                cols = slice(n * SPAN, (n + 1) * SPAN)
                nc.vector.quantize_mx(out=ycodes[G][:, cols].bitcast(FP8X4), scales=yscales[G][:, cols], in_=ybs[u][:])
            elif k == "y":
                u, G, n, t = op[1:3], int(op[1]), int(op[2]), int(op[3])
                dst = out_0[G * SPAN:(G + 1) * SPAN, n * SPAN:(n + 1) * SPAN].rearrange("(p t) m -> p t m", t=PACK)
                nc.sync.dma_start(out=dst[:, t, :], in_=ys[u][:, t, :])
            elif k == "r":
                u, G, n, h = op[1:3], int(op[1]), int(op[2]), int(op[3])
                cols = slice(n * SPAN + h * 256, n * SPAN + (h + 1) * 256)
                nc.vector.quantize_mx(out=ycodes[G][:, cols].bitcast(FP8X4), scales=yscales[G][:, cols],
                                      in_=ybs[u][:, h * 1024:(h + 1) * 1024])
            elif k in "Ww":
                G = int(op[1])
                lo, hi = 0, SAMP
                if op == "W2a":
                    lo, hi = 0, 768
                elif len(op) > 2:
                    lo, hi = int(op[2]) * SPAN, (int(op[2]) + 1) * SPAN
                if len(op) > 3:
                    lo, hi = lo + int(op[3]) * 256, lo + (int(op[3]) + 1) * 256
                dst = out_1[G].rearrange("p m t -> p (m t)")[:, lo * PACK:hi * PACK]
                nc.sync.dma_start(out=dst.bitcast(I32), in_=ycodes[G][:, lo:hi].bitcast(I32))
            elif op == "Z01":
                for q in range(4):
                    nc.sync.dma_start(out=out_2[0:2, 4 * q:4 * q + 4, :].rearrange("g r m -> r g m").bitcast(I32),
                                      in_=ysc01[32 * q:32 * q + 4, :, :].bitcast(I32))
            elif op == "Z2":
                for q in range(4):
                    nc.scalar.dma_start(out=out_2[2, 4 * q:4 * q + 4, :].bitcast(I32),
                                        in_=ysc2[32 * q:32 * q + 4, :].bitcast(I32))

        queues = {"D": DQ, "V": VQ, "S": SQ, "P": PQ}
        at = {e: 0 for e in queues}
        done = set()
        while any(at[e] < len(queues[e]) for e in queues):
            moved = False
            for e in queues:
                if at[e] < len(queues[e]) and all(d in done for d in needs(queues[e][at[e]])):
                    op = queues[e][at[e]]
                    emit(op, e)
                    done.add(op)
                    at[e] += 1
                    moved = True
            assert moved
